import numpy as np
import ml_dtypes

BF16 = ml_dtypes.bfloat16


def bf(x):
    return np.asarray(x, np.float32).astype(BF16)


def f32(x):
    return np.asarray(x, np.float32)


def f64(x):
    return np.asarray(x).astype(np.float64)


def striped(idx):
    return np.tile(idx.reshape(-1, 16).T, (8, 1))


def rows(idx, k):
    return np.tile(idx, (k, 1))


def look(tab, idx):
    return np.take_along_axis(f64(tab), rows(idx, len(tab)), axis=1)


K, S, D, V, N, M = 128, 256, 2, 128, 256, 512


def setup_inputs():
    return {"tab": f32(np.random.standard_normal((K, S))), "ctr": f32(np.random.standard_normal((K, V))), "w": bf(np.random.standard_normal((K, M)) / np.sqrt(K)), "b": f32(0.5 * np.random.standard_normal((M, 1))), "offs": striped(np.random.permutation(S)[:N])}


def reference(tab, ctr, w, b, offs):
    idx = offs[:16].T.reshape(-1)
    x = sum(np.maximum(look(tab, idx[d * V:(d + 1) * V]) - f64(ctr), 0.0) for d in range(D))
    y = f64(w).T @ x
    return np.maximum(y + f64(b), 0.0)

@@ -1,0 +1,47 @@
+import concourse.mybir as mybir
+
+F32, BF16, U16 = mybir.dt.float32, mybir.dt.bfloat16, mybir.dt.uint16
+ALU = mybir.AluOpType
+RELU = mybir.ActivationFunctionType.Relu
+
+R, S, D, N, M = 128, 256, 2, 128, 512
+COLUMNS = N // 16
+BLOCKS = M // 128
+FLOPS = 2 * R * M * N + 3 * D * R * N + 2 * M * N
+
+
+def tile_lookup_edge_sub_relu_kernel(tc, tab, ctr, w, b, offs, out):
+    nc = tc.nc
+    with tc.tile_pool(name="held", bufs=1) as held, tc.psum_pool(name="psum", bufs=1) as psum:
+        offsets = held.tile([128, D * COLUMNS], U16)
+        table = held.tile([R, S], F32)
+        centre = held.tile([R, N], F32)
+        weights = held.tile([R, M], BF16)
+        bias = held.tile([128, BLOCKS], F32)
+        nc.sync.dma_start(offsets[:], offs)
+        nc.scalar.dma_start(table[:], tab)
+        nc.sync.dma_start(centre[:], ctr)
+        nc.scalar.dma_start(weights[:], w)
+        nc.sync.dma_start(bias[:], b.rearrange("(p q) one -> p (q one)", q=BLOCKS))
+
+        difference = [held.tile([R, N], F32, name=f"difference{d}") for d in range(D)]
+        for d in range(D):
+            piece = offsets[:, d * COLUMNS : (d + 1) * COLUMNS]
+            nc.vector.tensor_tensor(difference[d][:], table[:].indirect(piece), centre[:], ALU.subtract)
+
+        positive = held.tile([R, N], F32)
+        nc.scalar.activation(positive[:], difference[0][:], RELU)
+        x = held.tile([R, N], BF16)
+        nc.vector.scalar_tensor_tensor(x[:], difference[1][:], 0.0, positive[:], ALU.max, ALU.add)
+
+        by_block = weights[:].rearrange("r (p q) -> r q p", q=BLOCKS)
+        result = held.tile([128, BLOCKS * N], F32)
+        for q in range(BLOCKS):
+            product = psum.tile([128, N], F32, name=f"product{q}")
+            nc.tensor.matmul(product[:], by_block[:, q, :], x[:], start=True, stop=True)
+            columns = result[:, q * N : (q + 1) * N]
+            if q % 2 == 0:
+                nc.vector.tensor_scalar(columns, product[:], bias[:, q : q + 1], 0.0, ALU.add, ALU.max)
+            else:
+                nc.scalar.activation(columns, product[:], RELU, bias=bias[:, q : q + 1])
+        nc.sync.dma_start(out.rearrange("(p q) j -> p (q j)", q=BLOCKS), result[:])

@@ -7,6 +7,7 @@ RELU = mybir.ActivationFunctionType.Relu
 R, S, D, N, M = 128, 256, 2, 128, 512
 COLUMNS = N // 16
 BLOCKS = M // 128
+WARM_UP = 6
 FLOPS = 2 * R * M * N + 3 * D * R * N + 2 * M * N
 
 
@@ -24,6 +25,12 @@ def tile_lookup_edge_sub_relu_kernel(tc, tab, ctr, w, b, offs, out):
         nc.scalar.dma_start(weights[:], w)
         nc.sync.dma_start(bias[:], b.rearrange("(p q) one -> p (q one)", q=BLOCKS))
 
+        zeros = held.tile([128, 512], BF16)
+        nc.gpsimd.memset(zeros[:], 0.0)
+        unread = psum.tile([128, 512], F32)
+        for i in range(WARM_UP):
+            nc.tensor.matmul(unread[:], zeros[:, :128], zeros[:], start=True, stop=True)
+
         difference = [held.tile([R, N], F32, name=f"difference{d}") for d in range(D)]
         for d in range(D):
             piece = offsets[:, d * COLUMNS : (d + 1) * COLUMNS]
@@ -35,13 +42,17 @@ def tile_lookup_edge_sub_relu_kernel(tc, tab, ctr, w, b, offs, out):
         nc.vector.scalar_tensor_tensor(x[:], difference[1][:], 0.0, positive[:], ALU.max, ALU.add)
 
         by_block = weights[:].rearrange("r (p q) -> r q p", q=BLOCKS)
-        result = held.tile([128, BLOCKS * N], F32)
-        for q in range(BLOCKS):
-            product = psum.tile([128, N], F32, name=f"product{q}")
-            nc.tensor.matmul(product[:], by_block[:, q, :], x[:], start=True, stop=True)
-            columns = result[:, q * N : (q + 1) * N]
-            if q % 2 == 0:
-                nc.vector.tensor_scalar(columns, product[:], bias[:, q : q + 1], 0.0, ALU.add, ALU.max)
-            else:
-                nc.scalar.activation(columns, product[:], RELU, bias=bias[:, q : q + 1])
-        nc.sync.dma_start(out.rearrange("(p q) j -> p (q j)", q=BLOCKS), result[:])
+        by_partition = out.rearrange("(p q) j -> p q j", q=BLOCKS)
+        half = BLOCKS // 2
+        first = held.tile([128, half, N], F32)
+        second = held.tile([128, half, N], F32)
+        for i in range(half):
+            product_v = psum.tile([128, N], F32, name=f"product_v{i}")
+            nc.tensor.matmul(product_v[:], by_block[:, i, :], x[:], start=True, stop=True)
+            nc.vector.tensor_scalar(first[:, i, :], product_v[:], bias[:, i : i + 1], 0.0, ALU.add, ALU.max)
+            q = half + i
+            product_s = psum.tile([128, N], F32, name=f"product_s{i}")
+            nc.tensor.matmul(product_s[:], by_block[:, q, :], x[:], start=True, stop=True)
+            nc.scalar.activation(second[:, i, :], product_s[:], RELU, bias=bias[:, q : q + 1])
+        nc.sync.dma_start(by_partition[:, :half, :], first[:])
+        nc.scalar.dma_start(by_partition[:, half:, :], second[:])

import concourse.mybir as mybir

F32, BF16, U16 = mybir.dt.float32, mybir.dt.bfloat16, mybir.dt.uint16
ALU = mybir.AluOpType
RELU = mybir.ActivationFunctionType.Relu

R, S, D, N, M = 128, 256, 2, 128, 512
COLUMNS = N // 16
BLOCKS = M // 128
WARM_UP = 6
FLOPS = 2 * R * M * N + 3 * D * R * N + 2 * M * N


def tile_lookup_edge_sub_relu_kernel(tc, tab, ctr, w, b, offs, out):
    nc = tc.nc
    with tc.tile_pool(name="held", bufs=1) as held, tc.psum_pool(name="psum", bufs=1) as psum:
        offsets = held.tile([128, D * COLUMNS], U16)
        table = held.tile([R, S], F32)
        centre = held.tile([R, N], F32)
        weights = held.tile([R, M], BF16)
        bias = held.tile([128, BLOCKS], F32)
        nc.sync.dma_start(offsets[:], offs)
        nc.scalar.dma_start(table[:], tab)
        nc.sync.dma_start(centre[:], ctr)
        nc.scalar.dma_start(weights[:], w)
        nc.sync.dma_start(bias[:], b.rearrange("(p q) one -> p (q one)", q=BLOCKS))

        zeros = held.tile([128, 512], BF16)
        nc.gpsimd.memset(zeros[:], 0.0)
        unread = psum.tile([128, 512], F32)
        for i in range(WARM_UP):
            nc.tensor.matmul(unread[:], zeros[:, :128], zeros[:], start=True, stop=True)

        difference = [held.tile([R, N], F32, name=f"difference{d}") for d in range(D)]
        for d in range(D):
            piece = offsets[:, d * COLUMNS : (d + 1) * COLUMNS]
            nc.vector.tensor_tensor(difference[d][:], table[:].indirect(piece), centre[:], ALU.subtract)

        positive = held.tile([R, N], F32)
        nc.scalar.activation(positive[:], difference[0][:], RELU)
        x = held.tile([R, N], BF16)
        nc.vector.scalar_tensor_tensor(x[:], difference[1][:], 0.0, positive[:], ALU.max, ALU.add)

        by_block = weights[:].rearrange("r (p q) -> r q p", q=BLOCKS)
        by_partition = out.rearrange("(p q) j -> p q j", q=BLOCKS)
        half = BLOCKS // 2
        first = held.tile([128, half, N], F32)
        second = held.tile([128, half, N], F32)
        for i in range(half):
            product_v = psum.tile([128, N], F32, name=f"product_v{i}")
            nc.tensor.matmul(product_v[:], by_block[:, i, :], x[:], start=True, stop=True)
            nc.vector.tensor_scalar(first[:, i, :], product_v[:], bias[:, i : i + 1], 0.0, ALU.add, ALU.max)
            q = half + i
            product_s = psum.tile([128, N], F32, name=f"product_s{i}")
            nc.tensor.matmul(product_s[:], by_block[:, q, :], x[:], start=True, stop=True)
            nc.scalar.activation(second[:, i, :], product_s[:], RELU, bias=bias[:, q : q + 1])
        nc.sync.dma_start(by_partition[:, :half, :], first[:])
        nc.scalar.dma_start(by_partition[:, half:, :], second[:])
